import numpy as np, ml_dtypes
CORES = [2,6,10,14,18,22,26,30]
N = 8
import mx_ref
BF = ml_dtypes.bfloat16
def gentries(a):
    return np.ascontiguousarray(a.reshape(8, 16, -1).transpose(0, 2, 1)).reshape(8, -1)
def gtable(e):
    e = np.asarray(e); return np.ascontiguousarray(e.reshape(8, -1, 16).transpose(0, 2, 1)).reshape(128, -1).astype(np.int32)
def gcols(t, e):
    v = np.concatenate([t.reshape(8, 16, -1, 4), np.zeros((8, 16, 1, 4), BF)], axis=2)
    return np.ascontiguousarray(np.stack([v[g][:, e[g]] for g in range(8)])).reshape(128, -1)
def pick(q, e):
    c = np.concatenate([q[0].reshape(128, -1, 4), np.zeros((128, 1, 4), np.uint8)], axis=1); s = np.concatenate([q[1], np.ones((16, 1), np.uint8)], axis=1)
    return (np.ascontiguousarray(c[:, e].reshape(128, -1)), np.ascontiguousarray(s[:, e]))
def join(*qs):
    return (np.concatenate([q[0] for q in qs], axis=1), np.concatenate([q[1] for q in qs], axis=1))
def put(q, e, v):
    c, s = q[0].reshape(128, -1, 4).copy(), q[1].copy(); c[:, e] = v[0].reshape(128, -1, 4); s[:, e] = v[1]
    return (c.reshape(128, -1), s)
def pk(c, s):
    return (np.ascontiguousarray(c), mx_ref.live(s))
def emit(q):
    return q[0], q[1]
def packed(v, rng):
    q = [mx_ref.quantize(np.ascontiguousarray(v[r])) for r in range(N)]
    return np.stack([a for a, b in q]), np.stack([mx_ref.plane(b, rng) for a, b in q])
def values_of_codes():
    e, c = np.zeros((128, 128, 4), np.float32), np.zeros((128, 2, 4), np.uint8)
    e[np.arange(128), np.arange(128), 0] = 1
    c[:127, :, 0] = np.arange(256).reshape(2, 128).T[:127]
    return mx_ref.matmul(mx_ref.quantize(e.reshape(128, 512).astype(BF)), (c.reshape(128, 8), np.full((16, 2), 127, np.uint8))).T.reshape(-1).astype(np.float64)
CODE_VALUE, SCALE_VALUE = values_of_codes(), 2.0 ** (np.arange(256) - 127.0)
def decode(q):
    return (CODE_VALUE[q[0]].reshape(16, 8, -1, 4) * SCALE_VALUE[q[1]][:, None, :, None] + 0.0).reshape(128, -1).astype(np.float32)
def f(rng, *shape):
    return mx_ref.flush((rng.standard_normal(shape, dtype=np.float32) * np.exp2(rng.integers(-2, 3, shape[:-1] + (1,)))).astype(BF))
def wide(rng, *shape, cols=0):
    v = rng.standard_normal(shape, dtype=np.float32) * np.exp2(rng.integers(-12, 13, shape)).astype(np.float32)
    if cols: v *= np.repeat(np.exp2(rng.integers(-cols, cols + 1, shape[:-2] + (1, shape[-1] // 4))) * (rng.random(shape[:-2] + (1, shape[-1] // 4)) > 0.0625), 4, axis=-1).astype(np.float32)
    return mx_ref.flush(v.astype(BF))
C, M, R = 256, 128, 3
def numbers_of(rng):
    return {"x": np.array(f(rng, N, 128, 4 * C)), "u": np.array(f(rng, N, 128, 512)), "v": np.array(f(rng, N, 128, 512))}
def shuffled(rng):
    return np.argsort(rng.random((N, 8, C)), axis=2)
def stored(t):
    return {"cf": np.stack([gtable(t[r]) for r in range(N)])}
def weights(rng, w):
    c, p = packed(np.ascontiguousarray(w).reshape(N, 128, 2048), rng)
    return {"wc": c, "ws": p}
def layers(rng, still=[]):
    w = np.array(f(rng, N, 128, 2048)).reshape(N, 8, 16, 4, 8, 16, 4)
    for i in still:
        w[:, :, i] = 0
        w[:, :, :, :, :, i] = 0
    return weights(rng, w)
def setup_inputs(rng):
    return {**numbers_of(rng), **stored(shuffled(rng)), **layers(rng)}
def setup_inputs_ties(rng):
    d = numbers_of(rng)
    x = d["x"].reshape(N, 8, 16, C, 4)
    x[:, :, :2] = 0
    x[:, :, 0, :, 0] = rng.integers(0, 4, (N, 8, C)).astype(np.float32).astype(BF)
    x[:, :, 1, :, 0] = rng.integers(0, 3, (N, 8, C)).astype(np.float32).astype(BF)
    u = d["u"].reshape(N, 128, 128, 4)
    u[:, :, ::16] = 0
    u[:, :, 1] = 0
    o = rng.permutation(N)
    for r in range(N):
        s = 0.0 if r == o[0] else -1.0 if r == o[1] else 1.0
        for h in range(0, 128, 16): u[r, h, h, 0] = s
        u[r, 1, 1, 0] = s
    return {"x": x.reshape(N, 128, 4 * C), "u": u.reshape(N, 128, 512), "v": d["v"], **stored(shuffled(rng)), **layers(rng, [0, 1])}
def setup_inputs_near(rng):
    d = numbers_of(rng)
    o = rng.permutation(N) % 4
    c = np.where(o % 2 == 0, 1.0, -1.0)
    x = d["x"].astype(np.float32).reshape(N, 8, 16, C, 4)
    x[:, :, 0] = 0
    x[:, :, 8:] = 0
    x[:, :, 0, :, 0] = c[:, None, None]
    s = rng.integers(0, 16, (N, 8, C))
    x[:, :, 8] = ((s[:, :, :, None] >> np.arange(4)) & 1) * np.exp2(np.arange(4) - 23.0)
    x[:, :, 11, :, 0] = 2.0 ** -10
    u = d["u"].reshape(N, 128, 128, 4)
    u[:, :, ::16] = 0
    u[:, :, 1] = 0
    for r in range(N):
        for g in 1 + rng.permutation(7)[:4]: x[r, g, 0, rng.integers(C), 0] = c[r] * 2.0 ** 29
        if o[r] == 1: x[r, 0, 0, rng.integers(C), 0] = -2.0 ** 29
        if o[r] == 3:
            i = rng.integers(0, 2, (8, C))
            x[r, :, 8:] = 0
            x[r, :, 10, :, 0] = (1.0 + 0.125 * i) * 2.0 ** -30
            x[r, :, 12, :, 0] = (1.125 - 0.125 * i) * 2.0 ** -30
        k = 2.0 ** -30 if o[r] == 2 else 1.0
        for a, h in [(0, 1)] + [(h, h) for h in range(0, 128, 16)]:
            if o[r] == 3:
                u[r, a + 10, h, 0] = 1.125 * 2.0 ** -30
                u[r, a + 12, h, 0] = 2.0 ** -30
            else:
                u[r, a, h, 0] = k
                u[r, a + 8, h] = k
                u[r, a + 11, h, 0] = k
    return {"x": x.reshape(N, 128, 4 * C).astype(BF), "u": u.reshape(N, 128, 512), "v": d["v"], **stored(shuffled(rng)), **layers(rng, [0] + [8, 9, 10, 11, 12, 13, 14, 15])}
def swings(rng):
    h, j, a = np.zeros(C, int), 0, 200
    while j < C:
        i = np.arange(min(int(rng.integers(10, 25)), C - j))
        n = np.where((i > 8) & (rng.random(len(i)) < 0.25), rng.integers(2, np.maximum(i, 3)), i)
        h[j:j + len(i)] = (1 - 2 * (i % 2)) * (a - 8 * n)
        j, a = j + len(i), a + 1
    return h
def setup_inputs_deep(rng):
    d = numbers_of(rng)
    x = d["x"].reshape(N, 8, 16, C, 4)
    o = rng.permutation(N)
    t = np.arange(C) - C // 2
    small = (1.0 + (2 * rng.integers(0, 64, (N, 8, 8, C, 4)) + 1) * 2.0 ** -7) * np.exp2(-rng.integers(8, 15, (N, 8, 8, C, 4)).astype(np.float64))
    small = small * rng.choice([-1.0, 1.0], small.shape)
    small[:, :, 0, :, 0] = np.where(rng.random((N, 8, C)) < 0.5, 1.875, 1.96875)
    x[:, :, 8:] = small.astype(np.float32).astype(BF)
    x[:, 0, 0] = 0
    u = d["u"].reshape(N, 128, 128, 4)
    u[:, :, 1] = 0
    u[:, 0, 1, 0] = 16
    u[:, 0, 1, 1] = 1
    for r in range(N):
        h = t if r == o[0] else -t if r == o[1] else swings(rng)
        x[r, 0, 0, :, 0] = (np.sign(h) * (np.abs(h) // 16)).astype(np.float32).astype(BF)
        x[r, 0, 0, :, 1] = (np.sign(h) * (np.abs(h) % 16)).astype(np.float32).astype(BF)
    return {"x": x.reshape(N, 128, 4 * C), "u": u.reshape(N, 128, 512), "v": d["v"], **stored(shuffled(rng)), **layers(rng)}
def setup_inputs_ends(rng):
    d = numbers_of(rng)
    o = (np.arange(N) + int(rng.integers(N))) % 4
    x = np.zeros((N, 8, 16, C, 4))
    u = d["u"].reshape(N, 128, 128, 4)
    u[:, :, ::16] = 0
    t = shuffled(rng)
    w = np.zeros((N, 128, 4, 128, 4), np.float32)
    i = np.arange(128)
    for r in range(N):
        sign = rng.permutation(8) % 2 * 2.0 - 1.0
        wave = 2.0 ** 30 * (0.9 + 0.1 * rng.random((128, 8, 4)))
        u[r, :, 1] = 2.0 ** -30 if o[r] == 3 else 2.0 ** 30
        if o[r] == 0:
            x[r] = -2.0 ** 30 * (0.9 + 0.1 * rng.random((8, 16, C, 4)))
            u[r, :, ::16] = wave.astype(np.float32).astype(BF)
            t[r] = np.arange(C)
        if o[r] == 1:
            x[r] = 2.0 ** 30 * np.where(rng.random((8, 16, C, 4)) < 0.125, 0.8125, 0.875) * (rng.permutation(C) % 2 * 2.0 - 1.0)[:, None]
            u[r, :, ::16] = (wave * sign[:, None]).astype(np.float32).astype(BF)
            for b in range(4): w[r, i, b, i, b] = rng.choice([-1.0, 1.0], 128)
        if o[r] == 2:
            x[r] = 2.0 ** 30
            x[r, rng.permutation(8)[:4]] *= np.where(rng.random((4, 1, C, 1)) < 0.5, 0.875, 1.0)
            t[r] = np.arange(C)[::-1]
            for g in range(8): u[r, 16 * g:16 * g + 16, 16 * g] = sign[g] * 2.0 ** 30
        if o[r] == 3:
            x[r] = 2.0 ** -30 * (1.0 + 0.125 * rng.integers(0, 8, (8, 16, C, 4)))
            t[r, ::2] = np.arange(C)
            t[r, 1::2] = np.arange(C)[::-1]
            for g in range(8): u[r, 16 * g:16 * g + 16, 16 * g] = 2.0 ** -30
    d["v"] = (np.where(d["v"] < 0, -1.0, 1.0) * np.where(rng.permutation(N) % 2, 2.0 ** -30, 2.0 ** 30)[:, None, None]).astype(np.float32).astype(BF)
    return {"x": x.astype(np.float32).reshape(N, 128, 4 * C).astype(BF), "u": u.reshape(N, 128, 512), "v": d["v"], **stored(t), **weights(rng, w.astype(BF))}
def setup_inputs_spread(rng):
    d = setup_inputs(rng)
    d["x"] = wide(rng, N, 128, 4 * C, cols=6)
    return d
def check_inputs(d):
    b = []
    for k in ("x", "u", "v"):
        a = np.abs(d[k].astype(np.float32))
        if not (np.isfinite(a).all() and ((a == 0) | (a >= 2.0 ** -30) & (a <= 2.0 ** 30)).all()): b.append("a value of " + k)
    none, least, most = [emit(mx_ref.quantize(np.full((128, 16), k, np.float32).astype(BF)))[1][0, 0] for k in (0.0, 2.0 ** -30, 2.0 ** 30)]
    for r in range(N):
        if (np.sort(gentries(d["cf"][r]), axis=1) != np.arange(C)).any(): b.append("cf: a group hasn't every column once")
        if ((d["wc"][r] == 0x7F) | (d["wc"][r] == 0xFF)).any(): b.append("wc: a code that is no number")
        s = mx_ref.live(d["ws"][r])
        if ((s != none) & ((s < least) | (s > most))).any(): b.append("ws: a scale out of range")
    return b
def turning(h):
    t = np.arange(C)
    e, found = np.zeros(C, np.int64), []
    for i in range(7):
        inside = (t >= e[:, None]) & (t <= t[:, None])
        s = np.where(inside, h if i % 2 == 0 else -h, np.float32(-np.inf))
        e = C - 1 - np.argmax(s[:, ::-1], axis=1)
        found.append(e)
    found = np.stack(found + [t])
    return found, np.argmax(found == t, axis=0)
def reference(x, u, v, cf, wc, ws):
    qu = [mx_ref.quantize(u[r]) for r in range(N)]
    lay = [pk(wc[r], ws[r]) for r in range(N)]
    now = [x[r] for r in range(N)]
    reads = [gentries(cf[r]) for r in range(N)]
    for t in range(R):
        blend, low, sent = [], [], []
        for r in range(N):
            q = mx_ref.quantize(now[r])
            own = decode(q).astype(BF)
            s = mx_ref.matmul(qu[r], q) + np.float32(0.0)
            e, depth = turning(s[1])
            at = np.take_along_axis(e, np.maximum(depth - np.arange(9)[:, None], 0), axis=0)
            a = np.take_along_axis(reads[r], at[:8], axis=1)
            b = np.take_along_axis(reads[r], at[1:], axis=1)
            z = ((gcols(own, a).astype(np.float32) + gcols(own, b).astype(np.float32)) * np.float32(0.5)).astype(BF)
            o = np.argsort(-s[::16], axis=1, kind="stable")
            l, d = o[:, :M], o[:, C - M:]
            sent.append(mx_ref.quantize(gcols(z, l)))
            other = np.tile(np.arange(C), (8, 1))
            np.put_along_axis(other, l, d, axis=1)
            np.put_along_axis(other, d, l, axis=1)
            reads[r] = np.take_along_axis(other, reads[r], axis=1)
            blend.append(z)
            low.append(d)
        for r in range(N):
            came = sent[(r - 1) % N]
            made = np.stack([mx_ref.matmul(pick(lay[r], np.arange(128 * b, 128 * b + 128)), came) * np.float32(0.03125) for b in range(4)], axis=2).reshape(8, 16, M, 4)
            z = blend[r].astype(np.float32).reshape(8, 16, C, 4)
            for g in range(8): z[g][:, low[r][g]] = made[g] + z[g][:, low[r][g]]
            now[r] = z.reshape(128, 4 * C).astype(BF)
    y, op = np.zeros((N, 128, C), np.float32), np.zeros((N, 8, C), np.float32)
    oc, osc = np.zeros((N, 128, 4 * C), np.uint8), np.zeros((N, 16, C), np.uint8)
    for r in range(N):
        q = mx_ref.quantize(now[r])
        y[r] = mx_ref.matmul(mx_ref.quantize(v[r]), q)
        op[r] = reads[r]
        oc[r], osc[r] = emit(q)
    return {"y": y, "op": op, "oc": oc, "osc": osc}

@@ -1,0 +1,385 @@
+from concourse.mybir import dt, AluOpType as A, ActivationFunctionType as AF
+
+ROUNDS = 3
+ZC = 384
+WIN = 400
+SPLIT, L1, L2 = 4, 3, 6
+
+SCRATCH = {}
+PSUM = ["p%d" % i for i in range(8)]
+for _n in PSUM:
+    SCRATCH[_n] = ("psum", [128, 512], "float32")
+for _n, _c in [("u", 128), ("v", 128), ("w", 512), ("us", 384), ("x", 256), ("eb", 512), ("sa", 128), ("k", 128), ("hs", 128), ("h", 256),
+               ("w0", 256), ("w1", 256), ("w2", 256), ("w3", 256), ("eq", 256), ("kt1", 256), ("kt2", 256),
+               ("e0", 128), ("e1", 128), ("e2", 128), ("l0", 128), ("l1", 128), ("l2", 128)]:
+    SCRATCH["q" + _n] = ("sbuf", [128, _c], "float8_e4m3fn_x4")
+    SCRATCH["z" + _n] = ("sbuf", [128, _c], "uint8")
+for _d, _l in [("bfloat16", [("ut", 512), ("vt", 512), ("xt", 1024), ("xn", 1024), ("ebt", 528), ("half", 528), ("sat", 512), ("kt", 512), ("hst", 512),
+                             ("ht", 1024), ("eqt", 1024), ("w0t", 1024), ("w1t", 1024), ("w2t", 1024), ("w3t", 1024), ("kt1t", 1024), ("kt2t", 1024),
+                             ("rho", 256), ("st0", 256), ("st1", 256), ("f", 1024), ("fh", 1024), ("rk", WIN), ("orow", WIN), ("cw", WIN), ("sg", WIN),
+                             ("vr", 512), ("vo", 512), ("vf", 512), ("vc", 512), ("tr", 512), ("to", 512), ("tf", 512), ("tc", 512),
+                             ("r1", 256), ("r2", 128), ("r3", 64), ("nn", 256), ("mm", 256), ("cc", 256), ("irow", 256),
+                             ("ta", 1024), ("et", 512), ("lt", 512), ("l32", 512), ("v32", 1024)]),
+               ("float32", [("owna", 256), ("ownb", 256), ("crow", 256), ("ys", 256), ("fc", 16), ("nl", 16), ("rl", 16), ("ol", 32), ("cl", 16), ("da", 32), ("db", 32)]),
+               ("int32", [("ci", 32), ("cfi", 16), ("uli", 24)]),
+               ("uint16", [("ul", 24), ("dn", 32), ("od", 32), ("cd", 32), ("cu", 16), ("rku", 16), ("xo", 64), ("lab", 32)])]:
+    for _n, _c in _l:
+        SCRATCH[_n] = ("sbuf", [128, _c], _d)
+
+SEMAPHORES = ["cv", "cs", "ct", "cg", "left"] + ["ar%d" % t for t in range(ROUNDS)] + ["d%d" % i for i in range(20)]
+
+
+def rank_program(g, core, T, topo):
+    rank = T.rank_of(core)
+    if rank is None:
+        return
+    nxt = T.cores[(rank + 1) % len(T.cores)]
+    prv = T.cores[(rank - 1) % len(T.cores)]
+    Q = {"v": g.vector, "s": g.scalar, "t": g.tensor, "g": g, "y": g.sync}
+    SEM = {"v": "cv", "s": "cs", "t": "ct", "g": "cg"}
+    total = {}
+    know = {q: {} for q in Q}
+    acc = {}
+    dmas = [0]
+
+    def V(name, lo=0, hi=None, st=1, p0=0, p1=128):
+        return (name, lo, SCRATCH[name][1][1] if hi is None else hi, st, p0, p1)
+
+    def ap(v):
+        name, lo, hi, st, p0, p1 = v
+        c = slice(lo, hi) if st == 1 else slice(lo, hi, st)
+        return T[name][:, c] if (p0, p1) == (0, 128) else T[name][p0:p1, c]
+
+    def meet(a, b):
+        if a[4] >= b[5] or b[4] >= a[5] or a[1] >= b[2] or b[1] >= a[2]:
+            return False
+        return not (a[3] == b[3] and (a[1] - b[1]) % a[3])
+
+    def learn(k, more):
+        for s, n in more.items():
+            if k.get(s, 0) < n:
+                k[s] = n
+
+    def order(q, reads, writes):
+        for v, w in [(r, False) for r in reads] + [(r, True) for r in writes]:
+            for (o, ow, oq, sem, n, kn) in acc.get(v[0], []):
+                if v[0] in PSUM:
+                    if not (w or ow or oq != q):
+                        continue
+                elif not (w or ow) or not meet(v, o):
+                    continue
+                if know[q].get(sem, 0) < n:
+                    Q[q].wait_ge(T.sem[sem], n)
+                    learn(know[q], {sem: n})
+                    learn(know[q], kn)
+
+    def note(q, reads, writes, sem, n):
+        kn = dict(know[q])
+        for v, w in [(r, False) for r in reads] + [(r, True) for r in writes]:
+            L = acc.setdefault(v[0], [])
+            if w:
+                L[:] = [e for e in L if not (e[0][1] >= v[1] and e[0][2] <= v[2] and e[0][4] >= v[4] and e[0][5] <= v[5]
+                                             and (v[3] == 1 or (v[3] == e[0][3] and (v[1] - e[0][1]) % v[3] == 0)))]
+            L.append((v, w, q, sem, n, kn))
+
+    def run(q, call, reads, writes, first=True):
+        order(q, reads, writes if first else [])
+        sem = SEM[q]
+        if q == "g" and know[q].get(sem, 0) < total.get(sem, 0):
+            g.wait_ge(T.sem[sem], total[sem])
+            know[q][sem] = total[sem]
+        call().then_inc(T.sem[sem], 1)
+        total[sem] = total.get(sem, 0) + 1
+        note(q, reads, writes, sem, total[sem])
+
+    def dma(q, out, in_, reads, writes):
+        order(q, reads, writes)
+        sem = "d%d" % dmas[0]
+        dmas[0] += 1
+        Q[q].dma_start(out, in_).then_inc(T.sem[sem], 16)
+        total[sem] = 16
+        note(q, reads, writes, sem, 16)
+
+    def ind(v, lst):
+        return ap(v) if lst is None else ap(v).indirect(ap(lst))
+
+    def some(*v):
+        return [x for x in v if isinstance(x, tuple)]
+
+    def col(s):
+        return ap(s) if isinstance(s, tuple) else s
+
+    def fill(v, c):
+        run("v", lambda: g.vector.memset(ap(v), c), [], [v])
+
+    def ts(out, in0, s1, s2, op0, op1=None, lst=None):
+        a = [ap(out), ind(in0, lst), col(s1), col(s2), op0] + ([] if op1 is None else [op1])
+        run("v", lambda: g.vector.tensor_scalar(*a), some(in0, s1, s2, lst), [out])
+
+    def tt(out, in0, in1, op, lst=None):
+        run("v", lambda: g.vector.tensor_tensor(ap(out), ind(in0, lst), ap(in1), op), some(in0, in1, lst), [out])
+
+    def scan(out, d0, d1, op0, op1):
+        run("v", lambda: g.vector.tensor_tensor_scan(ap(out), ap(d0), ap(d1), 0.0, op0, op1), [d0, d1], [out])
+
+    def copy(out, in_):
+        run("v", lambda: g.vector.tensor_copy(ap(out), ap(in_)), [in_], [out])
+
+    def act(out, in_, scale=1.0, lst=None, func=AF.Copy, bias=None):
+        k = {} if scale == 1.0 else {"scale": scale}
+        if bias is not None:
+            k["bias"] = ap(bias)
+        run("s", lambda: g.scalar.activation(ap(out), ind(in_, lst), func, **k), some(in_, lst, bias), [out])
+
+    def turn(out, in_):
+        run("v", lambda: g.vector.transpose(ap(out), ap(in_)), [in_], [out])
+
+    def quant(n, tile, lo=0, hi=None):
+        c, z = V("q" + n, lo, hi), V("z" + n, lo, hi)
+        run("v", lambda: g.vector.quantize_mx(ap(c), ap(z), ap(tile)), [tile], [c, z])
+
+    def mm(bank, cols, L, R, start=True, stop=True):
+        lc, lz = V("q" + L[0], L[1], L[1] + 128), V("z" + L[0], L[1], L[1] + 128)
+        rc, rz = V("q" + R[0], R[1], R[1] + cols), V("z" + R[0], R[1], R[1] + cols)
+        out = V(bank, 0, cols)
+        run("t", lambda: g.tensor.matmul_mx(ap(out), ap(lc), ap(lz), ap(rc), ap(rz), start, stop), [lc, lz, rc, rz], [out], start)
+
+    def listing(out, tile, turned):
+        turn(V(turned), V(tile))
+        tt(out, V(turned, 0, 512, 32), V(turned, 16, 512, 32), A.add)
+
+    def holes(out, lst):
+        ts(V(out, 0, 32, 2), lst, V("fc", 5, 6), V("fc", 6, 7), A.mult, A.add)
+        ts(V(out, 1, 32, 2), lst, V("fc", 4, 5), V("fc", 7, 8), A.mult, A.add)
+
+    dma("y", T["ut"][:, :], T.u[:, :], [], [V("ut")])
+    dma("s", T["xt"][:, 0:512], T.x[:, 0:512], [], [V("xt", 0, 512)])
+    dma("y", T["xt"][:, 512:1024], T.x[:, 512:1024], [], [V("xt", 512, 1024)])
+    dma("y", T["cfi"][:, :], T.cf[:, :], [], [V("cfi")])
+    dma("y", T["qw"][:, :].bitcast(dt.uint8), T.wc[:, :], [], [V("qw")])
+    dma("y", T["zw"][:, :], T.ws[:, :], [], [V("zw")])
+    dma("y", T["vt"][:, :], T.v[:, :], [], [V("vt")])
+
+    def iota(out, pattern, base, cm):
+        run("g", lambda: g.iota(ap(out), pattern, base, cm), [], [out])
+
+    iota(V("uli", 0, 8), [[32, 4], [0, 2]], 0, 0)
+    iota(V("uli", 8, 16), [[32, 4], [0, 2]], 16, 0)
+    iota(V("uli", 16, 24), [[0, 8]], 1, 0)
+    iota(V("ci", 0, 16), [[16, 16]], 0, 0)
+    iota(V("ci", 16, 17), [[0, 1]], 0, 1)
+    iota(V("ci", 17, 18), [[0, 1]], 8, 1)
+    fill(V("half"), 0.5)
+    run("g", lambda: g.affine_select(T["ebt"][:, :], T["half"][:, :], [[1, 528]], A.is_equal, 0.0, -4, -4), [V("half")], [V("ebt")])
+    run("g", lambda: g.iota(T["irow"][:, :], [[1, 256]], 0, 0, allow_small_or_imprecise_dtypes=True), [], [V("irow")])
+    fill(V("ht"), 0.0)
+    fill(V("hst"), 1.0 / 256)
+    fill(V("eqt"), 0.0)
+    copy(V("ul"), V("uli"))
+    quant("hs", V("hst"))
+    for n in ("rk", "orow", "cw", "sg"):
+        fill(V(n, 256, WIN), 0.0)
+    fill(V("kt2t", 3, 1024, 4), 0.0)
+    quant("u", V("ut"))
+    run("v", lambda: g.vector.tensor_copy(T["qus"][:, 0:384].bitcast(dt.uint32), T["qu"][:, 0:128].bitcast(dt.uint32).indirect(T["ul"][:, 0:24])), [V("qu"), V("ul")], [V("qus")])
+    run("s", lambda: g.scalar.activation(T["zus"][:, 0:384], T["zu"][:, 0:128].indirect(T["ul"][:, 0:24]), AF.Copy), [V("zu"), V("ul")], [V("zus")])
+
+    def constants():
+        fill(V("sat"), 0.0)
+        for a in range(4):
+            for b in range(4):
+                c = 128 * a + 64 * (b // 2)
+                fill(V("sat", c + b, c + 64, 4, 32 * a, 32 * a + 32), 1.0)
+        quant("sa", V("sat"))
+        fill(V("kt"), -1.0 / 128)
+        for b in (1, 3):
+            fill(V("kt", b, 512, 4), 1.0 / 128)
+        quant("k", V("kt"))
+        for b in range(4):
+            quant("eb", V("ebt", 4 - b, 516 - b), 128 * b, 128 * b + 128)
+        P, I, fc = V("ci", 16, 17), lambda i: V("ci", i, i + 1), lambda i: V("fc", i, i + 1)
+        ts(I(18), P, 7, None, A.bitwise_and)
+        ts(I(19), I(17), 4, None, A.arith_shift_right)
+        ts(I(21), P, 4, 1, A.arith_shift_right, A.bitwise_and)
+        ts(I(20), P, 15, None, A.bitwise_and)
+        ts(fc(0), I(18), -4.0, None, A.add)
+        ts(fc(1), I(19), -4.0, None, A.add)
+        copy(fc(4), I(21))
+        ts(fc(5), I(21), -1.0, 1.0, A.mult, A.add)
+        ts(fc(6), I(21), float(ZC), None, A.mult)
+        ts(fc(7), I(21), -float(ZC), float(ZC), A.mult, A.add)
+        copy(fc(8), I(20))
+        ts(fc(3), I(18), fc(1), None, A.add)
+        ts(V("nl"), V("ci", 0, 16), fc(8), None, A.add)
+        holes("dn", V("nl"))
+        copy(V("cu"), V("cfi"))
+        holes("cd", V("cfi"))
+
+    for t in range(ROUNDS):
+        last = t == ROUNDS - 1
+        quant("x", V("xt") if t == 0 else V("xn"))
+        for bank, c in (("p0", 0), ("p1", 128), ("p3", 0), ("p4", 128)):
+            mm(bank, 256, ("us", c), ("x", 0))
+        mm("p7", 128, ("x", 0), ("u", 0))
+        mm("p6", 128, ("x", 128), ("u", 0))
+        mm("p2", 256, ("us", 256), ("x", 0))
+        turn(V("owna"), V("p0", 0, 256))
+        turn(V("ownb"), V("p1", 0, 256))
+        tt(V("eqt", 0, 1024, 4), V("p0", 0, 256), V("owna"), A.is_equal)
+        tt(V("eqt", 2, 1024, 4), V("p1", 0, 256), V("ownb"), A.is_equal)
+        for b in range(2):
+            for a in range(4):
+                v = V("eqt", 2 * b, 1024, 4, 32 * a, 32 * a + 32)
+                run("g", lambda: g.affine_select(ap(v), ap(v), [[0, 8], [1, 32]], A.is_gt, 0.0, 0, -1), [v], [v])
+        ts(V("ht", 0, 1024, 4), V("p2", 0, 256), V("p7", 1, 2), None, A.is_gt)
+        ts(V("ht", 1, 1024, 4), V("p2", 0, 256), V("p6", 1, 2), None, A.is_gt)
+        quant("h", V("ht"))
+        mm("p2", 256, ("hs", 0), ("h", 0))
+        if t == 0:
+            constants()
+        for b in (0, 1):
+            mm(("p5", "p6")[b], 256, ("eb", 128 * b), ("x", 0))
+
+        def level(m):
+            S, flags = V("st%d" % (m % 2)), V("kt%dt" % (1 + m // 4), m % 4, 1024, 4)
+            if m == 0:
+                scan(S, V("rho"), V("rho"), A.max, A.max)
+            else:
+                ops = (A.max, A.min) if m % 2 else (A.min, A.max)
+                scan(S, V("kt%dt" % (1 + (m - 1) // 4), (m - 1) % 4, 1024, 4), V("rho"), ops[0], ops[1])
+            yield
+            tt(flags, V("p2", 0, 256), S, A.not_equal if m % 2 else A.is_equal)
+            yield
+            if m in (3, 6):
+                n = "kt%d" % (1 + m // 4)
+                quant(n, V(n + "t"))
+                mm("p0", 256, ("k", 0), (n, 0), m == 3, m == 6)
+
+        def levels(a, z):
+            for m in range(a, z):
+                for _ in level(m):
+                    yield
+
+        def rest(it):
+            for _ in it:
+                pass
+        ahead, n = levels(0, L1), 0
+        for b in list(range(SPLIT, 8)) + list(range(SPLIT)):
+            i = b // 2
+            tile = "w%dt" % i
+            for h in (0, 1):
+                own, e, c = V(("owna", "ownb")[h], 32 * b, 32 * b + 1), 32 * b + 32, b % 2 + 2 * h
+                left = V(tile, c, 4 * e, 4)
+                if b < SPLIT:
+                    ts(left, V(("p0", "p1")[h], 0, e), own, None, A.is_lt)
+                else:
+                    act(left, V(("p3", "p4")[h], 0, e), -1.0, None, AF.Relu, own)
+                if b < 7:
+                    ts(V(tile, 4 * e + c, 1024, 4), V(("p0", "p1")[h], e, 256), own, None, A.is_le)
+                if b < SPLIT:
+                    n += 1
+                    if n == 1:
+                        act(V("rho"), V("p2", 0, 256))
+                    elif n > 1:
+                        next(ahead, None)
+            if b % 2:
+                if b >= SPLIT:
+                    w = V(tile, 0, 4 * e)
+                    act(w, w, func=AF.Sign)
+                else:
+                    quant("w%d" % i, V(tile))
+                    mm("p7", 256, ("sa", 0), ("w%d" % i, 0), i == 0, False)
+        rest(ahead)
+        for b in range(SPLIT // 2, 4):
+            quant("w%d" % b, V("w%dt" % b))
+            mm("p7", 256, ("sa", 0), ("w%d" % b, 0), False, False)
+        quant("eq", V("eqt"))
+        mm("p7", 256, ("sa", 0), ("eq", 0), False, True)
+        act(V("rk", 0, 256), V("p7", 0, 256))
+        act(V("vr"), V("rk"), lst=V("dn"))
+        for b in (2, 3):
+            mm(("p3", "p4")[b - 2], 256, ("eb", 128 * b), ("x", 0))
+        for b, bank in enumerate(("p5", "p6", "p3", "p4")):
+            act(V("f", 256 * b, 256 * b + 256), V(bank, 0, 256))
+        rest(levels(L1, L2))
+        listing(V("rl"), "vr", "tr")
+        copy(V("rku"), V("rl"))
+        run("v", lambda: g.vector.tensor_copy(T["orow"][:, 0:256].indirect(T["rku"][:, :]), T["irow"][:, :]), [V("irow"), V("rku")], [V("orow", 0, 256)])
+        act(V("vo"), V("orow"), lst=V("dn"))
+        for b in range(4):
+            act(V("fh", 256 * b, 256 * b + 256), V("f", 256 * b, 256 * b + 256), lst=V("cu"))
+        rest(levels(L2, 7))
+        k = V("p0", 0, 256)
+        ts(V("nn"), k, V("fc", 0, 1), None, A.is_gt)
+        scan(V("cc"), V("nn"), V("nn"), A.mult, A.add)
+        ts(V("mm"), k, V("fc", 1, 2), V("fc", 3, 4), A.max, A.is_equal)
+        tt(V("cw", 0, 256), V("cc"), V("mm"), A.mult)
+        listing(V("ol", 0, 16), "vo", "to")
+        holes("od", V("ol", 0, 16))
+        for half in (0, 1):
+            act(V("vf", 256 * half, 256 * half + 256), V("cw"), lst=V("od", 16 * half, 16 * half + 16))
+        copy(V("ol", 16, 32), V("ol", 0, 16))
+        for b in range(4):
+            ts(V("xo", 16 * b, 16 * b + 16), V("rl"), 4.0, float(b), A.mult, A.add)
+        for half, tile in ((0, "et"), (1, "lt")):
+            a, z = 256 * half, 256 * half + 256
+            turn(V("tf", a, z), V("vf", a, z))
+            for o, i in (("r1", "tf"), ("r2", "r1"), ("r3", "r2")):
+                tt(V(o, a // 2, z // 2), V(i, a, z, 2), V(i, a + 1, z, 2), A.add)
+                a, z = a // 2, z // 2
+            p = 8 * half
+            for s in (0, 1):
+                tt(V("da", 16 * s + p, 16 * s + p + 8), V("r3", a + s, z, 4), V("r3", a + s + 2, z, 4), A.add)
+            for s in (0, 16):
+                tt(V("db", s + p, s + p + 8), V("ol", p, p + 8), V("da", s + p, s + p + 8), A.subtract)
+                copy(V("lab", s + p, s + p + 8), V("db", s + p, s + p + 8))
+            for b in range(4):
+                tmp = V("ta", 512 * half + 128 * b, 512 * half + 128 * b + 128)
+                F = V("fh", 256 * b, 256 * b + 256)
+                act(tmp, F, lst=V("lab", p, p + 8))
+                tt(V(tile, b, 512, 4), F, tmp, A.add, lst=V("lab", 16 + p, 24 + p))
+            if half == 0:
+                e = "e%d" % t
+                quant(e, V("et"))
+                order("g", [V("q" + e), V("z" + e)], [])
+                rid, pid = topo.addr(nxt)[:2]
+                m = topo.mask(core, nxt)
+                g.remote_dma(T["ql%d" % t][:, 0:128].bitcast(dt.uint8), T["q" + e][:, 0:128].bitcast(dt.uint8), T.sem["ar%d" % t], T.sem["left"], pid, rid, m)
+                g.remote_dma(T["zl%d" % t][:, 0:128], T["z" + e][:, 0:128], T.sem["ar%d" % t], T.sem["left"], pid, rid, m)
+                total["left"] = total.get("left", 0) + 2 * len(topo.engines(core, nxt))
+        ts(V("l32"), V("lt"), 32.0, None, A.mult)
+        ts(V("v32", 0, 512), V("et"), 32.0, None, A.mult)
+        act(V("orow", 256, 384), V("orow", 0, 128))
+        act(V("sg", 0, 256), V("orow", 128, 384), lst=V("rku"))
+        if last:
+            act(V("crow"), V("sg", 0, 256), lst=V("cu"))
+            dma("y", T.op[:, :], T["crow"][0:128:16, :], [V("crow")], [])
+            quant("v", V("vt"))
+        else:
+            act(V("vc"), V("sg"), lst=V("cd"))
+            listing(V("cl"), "vc", "tc")
+            copy(V("cu"), V("cl"))
+            holes("cd", V("cl"))
+        n = 2 * len(topo.engines(prv, core))
+        total["ar%d" % t] = n
+        for z in ("ql%d" % t, "zl%d" % t):
+            acc.setdefault(z, []).append((V(z), True, "r", "ar%d" % t, n, {}))
+        for b, bank in enumerate(("p0", "p1", "p7", "p3")):
+            mm(bank, 128, ("w", 128 * b), ("l%d" % t, 0))
+            tt(V("v32", 512 + b, 1024, 4), V(bank, 0, 128), V("l32", b, 512, 4), A.add)
+        for b in range(4):
+            out, win, lst = V("xn", b, 1024, 4), V("v32"), V("xo", 16 * b, 16 * b + 16)
+            if b % 2 == 0:
+                act(out, win, scale=0.03125, lst=lst)
+            else:
+                ts(out, win, 0.03125, None, A.mult, lst=lst)
+
+    quant("x", V("xn"))
+    mm("p4", 256, ("v", 0), ("x", 0))
+    act(V("ys"), V("p4", 0, 256))
+    dma("y", T.oc[:, :], T["qx"][:, :].bitcast(dt.uint8), [V("qx")], [])
+    for i in range(4):
+        dma("y" if i % 2 else "s", T.osc[4 * i:4 * i + 4, :], T["zx"][32 * i:32 * i + 4, :], [V("zx")], [])
+    dma("y", T.y[:, :], T["ys"][:, :], [V("ys")], [])
+    for sem, n in total.items():
+        g.wait_ge(T.sem[sem], n)

@@ -3,7 +3,7 @@ from concourse.mybir import dt, AluOpType as A, ActivationFunctionType as AF
 ROUNDS = 3
 ZC = 384
 WIN = 400
-SPLIT, L1, L2 = 4, 3, 6
+SPLIT, L1, L2 = 4, 3, 5
 
 SCRATCH = {}
 PSUM = ["p%d" % i for i in range(8)]
@@ -20,7 +20,7 @@ for _d, _l in [("bfloat16", [("ut", 512), ("vt", 512), ("xt", 1024), ("xn", 1024
                              ("vr", 512), ("vo", 512), ("vf", 512), ("vc", 512), ("tr", 512), ("to", 512), ("tf", 512), ("tc", 512),
                              ("r1", 256), ("r2", 128), ("r3", 64), ("nn", 256), ("mm", 256), ("cc", 256), ("irow", 256),
                              ("ta", 1024), ("et", 512), ("lt", 512), ("l32", 512), ("v32", 1024)]),
-               ("float32", [("owna", 256), ("ownb", 256), ("crow", 256), ("ys", 256), ("fc", 16), ("nl", 16), ("rl", 16), ("ol", 32), ("cl", 16), ("da", 32), ("db", 32)]),
+               ("float32", [("owna", 256), ("ownb", 256), ("crow", 256), ("ys", 256), ("fc", 16), ("nl", 16), ("rl", 16), ("ol", 16), ("cl", 16), ("da", 32), ("db", 32)]),
                ("int32", [("ci", 32), ("cfi", 16), ("uli", 24)]),
                ("uint16", [("ul", 24), ("dn", 32), ("od", 32), ("cd", 32), ("cu", 16), ("rku", 16), ("xo", 64), ("lab", 32)])]:
     for _n, _c in _l:
@@ -144,19 +144,21 @@ def rank_program(g, core, T, topo):
         out = V(bank, 0, cols)
         run("t", lambda: g.tensor.matmul_mx(ap(out), ap(lc), ap(lz), ap(rc), ap(rz), start, stop), [lc, lz, rc, rz], [out], start)
 
-    def listing(out, tile, turned):
-        turn(V(turned), V(tile))
+    def add_halves(out, turned):
         tt(out, V(turned, 0, 512, 32), V(turned, 16, 512, 32), A.add)
 
     def holes(out, lst):
         ts(V(out, 0, 32, 2), lst, V("fc", 5, 6), V("fc", 6, 7), A.mult, A.add)
         ts(V(out, 1, 32, 2), lst, V("fc", 4, 5), V("fc", 7, 8), A.mult, A.add)
 
+    def quarter(n, b):
+        return V(n, 256 * b, 256 * b + 256)
+
     dma("y", T["ut"][:, :], T.u[:, :], [], [V("ut")])
     dma("s", T["xt"][:, 0:512], T.x[:, 0:512], [], [V("xt", 0, 512)])
     dma("y", T["xt"][:, 512:1024], T.x[:, 512:1024], [], [V("xt", 512, 1024)])
     dma("y", T["cfi"][:, :], T.cf[:, :], [], [V("cfi")])
-    dma("y", T["qw"][:, :].bitcast(dt.uint8), T.wc[:, :], [], [V("qw")])
+    dma("y", T["qw"][:, :].bitcast(dt.uint8), T.wc[:, :], [V("ut"), V("xt")], [V("qw")])
     dma("y", T["zw"][:, :], T.ws[:, :], [], [V("zw")])
     dma("y", T["vt"][:, :], T.v[:, :], [], [V("vt")])
 
@@ -170,7 +172,13 @@ def rank_program(g, core, T, topo):
     iota(V("ci", 16, 17), [[0, 1]], 0, 1)
     iota(V("ci", 17, 18), [[0, 1]], 8, 1)
     fill(V("half"), 0.5)
+    fill(V("sat"), 0.0)
     run("g", lambda: g.affine_select(T["ebt"][:, :], T["half"][:, :], [[1, 528]], A.is_equal, 0.0, -4, -4), [V("half")], [V("ebt")])
+    for a in range(4):
+        for h in (0, 1):
+            c = 128 * a + 64 * h
+            o, i = V("sat", c, c + 64, 1, 32 * a, 32 * a + 32), V("half", c, c + 64, 1, 32 * a, 32 * a + 32)
+            run("g", lambda: g.affine_select(ap(o), ap(i), [[0, 16], [1, 2], [0, 2]], A.is_equal, 0.0, -h, 0), [i], [o])
     run("g", lambda: g.iota(T["irow"][:, :], [[1, 256]], 0, 0, allow_small_or_imprecise_dtypes=True), [], [V("irow")])
     fill(V("ht"), 0.0)
     fill(V("hst"), 1.0 / 256)
@@ -185,11 +193,6 @@ def rank_program(g, core, T, topo):
     run("s", lambda: g.scalar.activation(T["zus"][:, 0:384], T["zu"][:, 0:128].indirect(T["ul"][:, 0:24]), AF.Copy), [V("zu"), V("ul")], [V("zus")])
 
     def constants():
-        fill(V("sat"), 0.0)
-        for a in range(4):
-            for b in range(4):
-                c = 128 * a + 64 * (b // 2)
-                fill(V("sat", c + b, c + 64, 4, 32 * a, 32 * a + 32), 1.0)
         quant("sa", V("sat"))
         fill(V("kt"), -1.0 / 128)
         for b in (1, 3):
@@ -223,6 +226,9 @@ def rank_program(g, core, T, topo):
         mm("p7", 128, ("x", 0), ("u", 0))
         mm("p6", 128, ("x", 128), ("u", 0))
         mm("p2", 256, ("us", 256), ("x", 0))
+        if t:
+            turn(V("tc"), V("vc"))
+            add_halves(V("cl"), "tc")
         turn(V("owna"), V("p0", 0, 256))
         turn(V("ownb"), V("p1", 0, 256))
         tt(V("eqt", 0, 1024, 4), V("p0", 0, 256), V("owna"), A.is_equal)
@@ -237,6 +243,9 @@ def rank_program(g, core, T, topo):
         mm("p2", 256, ("hs", 0), ("h", 0))
         if t == 0:
             constants()
+        else:
+            copy(V("cu"), V("cl"))
+            holes("cd", V("cl"))
         for b in (0, 1):
             mm(("p5", "p6")[b], 256, ("eb", 128 * b), ("x", 0))
 
@@ -263,7 +272,7 @@ def rank_program(g, core, T, topo):
         def rest(it):
             for _ in it:
                 pass
-        ahead, n = levels(0, L1), 0
+        ahead = levels(0, L1)
         for b in list(range(SPLIT, 8)) + list(range(SPLIT)):
             i = b // 2
             tile = "w%dt" % i
@@ -277,12 +286,10 @@ def rank_program(g, core, T, topo):
                 if b < 7:
                     ts(V(tile, 4 * e + c, 1024, 4), V(("p0", "p1")[h], e, 256), own, None, A.is_le)
                 if b < SPLIT:
-                    n += 1
-                    if n == 1:
-                        act(V("rho"), V("p2", 0, 256))
-                    elif n > 1:
-                        next(ahead, None)
+                    next(ahead, None)
             if b % 2:
+                if b == SPLIT + 1:
+                    act(V("rho"), V("p2", 0, 256))
                 if b >= SPLIT:
                     w = V(tile, 0, 4 * e)
                     act(w, w, func=AF.Sign)
@@ -295,35 +302,48 @@ def rank_program(g, core, T, topo):
             mm("p7", 256, ("sa", 0), ("w%d" % b, 0), False, False)
         quant("eq", V("eqt"))
         mm("p7", 256, ("sa", 0), ("eq", 0), False, True)
-        act(V("rk", 0, 256), V("p7", 0, 256))
+        act(V("rk", 0, 256), V("p7", 0, 256), 2.0)
         act(V("vr"), V("rk"), lst=V("dn"))
         for b in (2, 3):
             mm(("p3", "p4")[b - 2], 256, ("eb", 128 * b), ("x", 0))
         for b, bank in enumerate(("p5", "p6", "p3", "p4")):
-            act(V("f", 256 * b, 256 * b + 256), V(bank, 0, 256))
+            act(quarter("f", b), V(bank, 0, 256))
         rest(levels(L1, L2))
-        listing(V("rl"), "vr", "tr")
+        more = levels(L2, 7)
+        next(more)
+        turn(V("tr"), V("vr"))
+        next(more)
+        add_halves(V("rl"), "tr")
+        next(more)
         copy(V("rku"), V("rl"))
+        rest(more)
         run("v", lambda: g.vector.tensor_copy(T["orow"][:, 0:256].indirect(T["rku"][:, :]), T["irow"][:, :]), [V("irow"), V("rku")], [V("orow", 0, 256)])
         act(V("vo"), V("orow"), lst=V("dn"))
         for b in range(4):
-            act(V("fh", 256 * b, 256 * b + 256), V("f", 256 * b, 256 * b + 256), lst=V("cu"))
-        rest(levels(L2, 7))
+            act(quarter("fh", b), quarter("f", b), lst=V("cu"))
+        act(V("orow", 256, 384), V("orow", 0, 128))
+        act(V("sg", 0, 256), V("orow", 128, 384), lst=V("rku"))
         k = V("p0", 0, 256)
         ts(V("nn"), k, V("fc", 0, 1), None, A.is_gt)
-        scan(V("cc"), V("nn"), V("nn"), A.mult, A.add)
         ts(V("mm"), k, V("fc", 1, 2), V("fc", 3, 4), A.max, A.is_equal)
+        scan(V("cc"), V("nn"), V("nn"), A.mult, A.add)
+        turn(V("to"), V("vo"))
         tt(V("cw", 0, 256), V("cc"), V("mm"), A.mult)
-        listing(V("ol", 0, 16), "vo", "to")
-        holes("od", V("ol", 0, 16))
+        add_halves(V("ol"), "to")
+        holes("od", V("ol"))
         for half in (0, 1):
             act(V("vf", 256 * half, 256 * half + 256), V("cw"), lst=V("od", 16 * half, 16 * half + 16))
-        copy(V("ol", 16, 32), V("ol", 0, 16))
+        if last:
+            act(V("crow"), V("sg", 0, 256), lst=V("cu"))
+            dma("y", T.op[:, :], T["crow"][0:128:16, :], [V("crow")], [])
+        else:
+            act(V("vc"), V("sg"), lst=V("cd"))
         for b in range(4):
             ts(V("xo", 16 * b, 16 * b + 16), V("rl"), 4.0, float(b), A.mult, A.add)
         for half, tile in ((0, "et"), (1, "lt")):
             a, z = 256 * half, 256 * half + 256
-            turn(V("tf", a, z), V("vf", a, z))
+            if half == 0:
+                turn(V("tf", a, z), V("vf", a, z))
             for o, i in (("r1", "tf"), ("r2", "r1"), ("r3", "r2")):
                 tt(V(o, a // 2, z // 2), V(i, a, z, 2), V(i, a + 1, z, 2), A.add)
                 a, z = a // 2, z // 2
@@ -332,12 +352,14 @@ def rank_program(g, core, T, topo):
                 tt(V("da", 16 * s + p, 16 * s + p + 8), V("r3", a + s, z, 4), V("r3", a + s + 2, z, 4), A.add)
             for s in (0, 16):
                 tt(V("db", s + p, s + p + 8), V("ol", p, p + 8), V("da", s + p, s + p + 8), A.subtract)
+            for s in (0, 16):
                 copy(V("lab", s + p, s + p + 8), V("db", s + p, s + p + 8))
+            if half == 0:
+                turn(V("tf", 256, 512), V("vf", 256, 512))
             for b in range(4):
                 tmp = V("ta", 512 * half + 128 * b, 512 * half + 128 * b + 128)
-                F = V("fh", 256 * b, 256 * b + 256)
-                act(tmp, F, lst=V("lab", p, p + 8))
-                tt(V(tile, b, 512, 4), F, tmp, A.add, lst=V("lab", 16 + p, 24 + p))
+                act(tmp, quarter("fh", b), lst=V("lab", p, p + 8))
+                tt(V(tile, b, 512, 4), quarter("fh", b), tmp, A.add, lst=V("lab", 16 + p, 24 + p))
             if half == 0:
                 e = "e%d" % t
                 quant(e, V("et"))
@@ -347,19 +369,10 @@ def rank_program(g, core, T, topo):
                 g.remote_dma(T["ql%d" % t][:, 0:128].bitcast(dt.uint8), T["q" + e][:, 0:128].bitcast(dt.uint8), T.sem["ar%d" % t], T.sem["left"], pid, rid, m)
                 g.remote_dma(T["zl%d" % t][:, 0:128], T["z" + e][:, 0:128], T.sem["ar%d" % t], T.sem["left"], pid, rid, m)
                 total["left"] = total.get("left", 0) + 2 * len(topo.engines(core, nxt))
+                act(V("v32", 0, 512), V("et"), 32.0)
         ts(V("l32"), V("lt"), 32.0, None, A.mult)
-        ts(V("v32", 0, 512), V("et"), 32.0, None, A.mult)
-        act(V("orow", 256, 384), V("orow", 0, 128))
-        act(V("sg", 0, 256), V("orow", 128, 384), lst=V("rku"))
         if last:
-            act(V("crow"), V("sg", 0, 256), lst=V("cu"))
-            dma("y", T.op[:, :], T["crow"][0:128:16, :], [V("crow")], [])
             quant("v", V("vt"))
-        else:
-            act(V("vc"), V("sg"), lst=V("cd"))
-            listing(V("cl"), "vc", "tc")
-            copy(V("cu"), V("cl"))
-            holes("cd", V("cl"))
         n = 2 * len(topo.engines(prv, core))
         total["ar%d" % t] = n
         for z in ("ql%d" % t, "zl%d" % t):
@@ -376,7 +389,7 @@ def rank_program(g, core, T, topo):
 
     quant("x", V("xn"))
     mm("p4", 256, ("v", 0), ("x", 0))
-    act(V("ys"), V("p4", 0, 256))
+    copy(V("ys"), V("p4", 0, 256))
     dma("y", T.oc[:, :], T["qx"][:, :].bitcast(dt.uint8), [V("qx")], [])
     for i in range(4):
         dma("y" if i % 2 else "s", T.osc[4 * i:4 * i + 4, :], T["zx"][32 * i:32 * i + 4, :], [V("zx")], [])

@@ -3,6 +3,7 @@ from concourse.mybir import dt, AluOpType as A, ActivationFunctionType as AF
 ROUNDS = 3
 ZC = 384
 WIN = 400
+XS = (0, 1)
 SPLIT, L1, L2 = 4, 3, 5
 
 SCRATCH = {}
@@ -20,9 +21,10 @@ for _d, _l in [("bfloat16", [("ut", 512), ("vt", 512), ("xt", 1024), ("xn", 1024
                              ("vr", 512), ("vo", 512), ("vf", 512), ("vc", 512), ("tr", 512), ("to", 512), ("tf", 512), ("tc", 512),
                              ("r1", 256), ("r2", 128), ("r3", 64), ("nn", 256), ("mm", 256), ("cc", 256), ("irow", 256),
                              ("ta", 1024), ("et", 512), ("lt", 512), ("l32", 512), ("v32", 1024)]),
-               ("float32", [("owna", 256), ("ownb", 256), ("crow", 256), ("ys", 256), ("fc", 16), ("nl", 16), ("rl", 16), ("ol", 16), ("cl", 16), ("da", 32), ("db", 32)]),
+               ("float32", [("owna", 256), ("ownb", 256), ("crow", 256), ("ys", 256), ("fc", 16), ("nl", 16), ("nf", 16),
+                            ("rl", 16), ("ol", 16), ("cl", 16), ("da", 32), ("db", 32)]),
                ("int32", [("ci", 32), ("cfi", 16), ("uli", 24)]),
-               ("uint16", [("ul", 24), ("dn", 32), ("od", 32), ("cd", 32), ("cu", 16), ("rku", 16), ("xo", 64), ("lab", 32)])]:
+               ("uint16", [("ul", 24), ("dn", 32), ("od", 32), ("cd", 32), ("cu", 16), ("rku", 16), ("lab", 32)])]:
     for _n, _c in _l:
         SCRATCH[_n] = ("sbuf", [128, _c], _d)
 
@@ -149,10 +151,16 @@ def rank_program(g, core, T, topo):
 
     def holes(out, lst):
         ts(V(out, 0, 32, 2), lst, V("fc", 5, 6), V("fc", 6, 7), A.mult, A.add)
-        ts(V(out, 1, 32, 2), lst, V("fc", 4, 5), V("fc", 7, 8), A.mult, A.add)
+        ts(V(out, 1, 32, 2), lst, V("fc", 9, 10), V("fc", 7, 8), A.mult, A.add)
 
     def quarter(n, b):
         return V(n, 256 * b, 256 * b + 256)
+
+    def I(i):
+        return V("ci", i, i + 1)
+
+    def fc(i):
+        return V("fc", i, i + 1)
 
     dma("y", T["ut"][:, :], T.u[:, :], [], [V("ut")])
     dma("s", T["xt"][:, 0:512], T.x[:, 0:512], [], [V("xt", 0, 512)])
@@ -168,9 +176,9 @@ def rank_program(g, core, T, topo):
     iota(V("uli", 0, 8), [[32, 4], [0, 2]], 0, 0)
     iota(V("uli", 8, 16), [[32, 4], [0, 2]], 16, 0)
     iota(V("uli", 16, 24), [[0, 8]], 1, 0)
-    iota(V("ci", 0, 16), [[16, 16]], 0, 0)
-    iota(V("ci", 16, 17), [[0, 1]], 0, 1)
-    iota(V("ci", 17, 18), [[0, 1]], 8, 1)
+    iota(I(16), [[0, 1]], 0, 1)
+    iota(I(17), [[0, 1]], 8, 1)
+    run("g", lambda: g.iota(T["nf"][:, :], [[16, 16]], 0, 0, allow_small_or_imprecise_dtypes=True), [], [V("nf")])
     fill(V("half"), 0.5)
     fill(V("sat"), 0.0)
     run("g", lambda: g.affine_select(T["ebt"][:, :], T["half"][:, :], [[1, 528]], A.is_equal, 0.0, -4, -4), [V("half")], [V("ebt")])
@@ -180,13 +188,16 @@ def rank_program(g, core, T, topo):
             o, i = V("sat", c, c + 64, 1, 32 * a, 32 * a + 32), V("half", c, c + 64, 1, 32 * a, 32 * a + 32)
             run("g", lambda: g.affine_select(ap(o), ap(i), [[0, 16], [1, 2], [0, 2]], A.is_equal, 0.0, -h, 0), [i], [o])
     run("g", lambda: g.iota(T["irow"][:, :], [[1, 256]], 0, 0, allow_small_or_imprecise_dtypes=True), [], [V("irow")])
-    fill(V("ht"), 0.0)
     fill(V("hst"), 1.0 / 256)
-    fill(V("eqt"), 0.0)
+    for b in (0, 1):
+        act(V("kt", b, 512, 2), V("hst", b, 512, 2), (-2.0, 2.0)[b])
+    fill(V("ht", 2, 1024, 4), 0.0)
+    fill(V("ht", 3, 1024, 4), 0.0)
+    fill(V("eqt", 1, 1024, 2), 0.0)
     copy(V("ul"), V("uli"))
     quant("hs", V("hst"))
-    for n in ("rk", "orow", "cw", "sg"):
-        fill(V(n, 256, WIN), 0.0)
+    for n, c in (("rk", 0.0), ("orow", float(ZC)), ("cw", 0.0), ("sg", float(ZC))):
+        fill(V(n, 256, WIN), c)
     fill(V("kt2t", 3, 1024, 4), 0.0)
     quant("u", V("ut"))
     run("v", lambda: g.vector.tensor_copy(T["qus"][:, 0:384].bitcast(dt.uint32), T["qu"][:, 0:128].bitcast(dt.uint32).indirect(T["ul"][:, 0:24])), [V("qu"), V("ul")], [V("qus")])
@@ -194,28 +205,21 @@ def rank_program(g, core, T, topo):
 
     def constants():
         quant("sa", V("sat"))
-        fill(V("kt"), -1.0 / 128)
-        for b in (1, 3):
-            fill(V("kt", b, 512, 4), 1.0 / 128)
         quant("k", V("kt"))
         for b in range(4):
             quant("eb", V("ebt", 4 - b, 516 - b), 128 * b, 128 * b + 128)
-        P, I, fc = V("ci", 16, 17), lambda i: V("ci", i, i + 1), lambda i: V("fc", i, i + 1)
-        ts(I(18), P, 7, None, A.bitwise_and)
-        ts(I(19), I(17), 4, None, A.arith_shift_right)
-        ts(I(21), P, 4, 1, A.arith_shift_right, A.bitwise_and)
-        ts(I(20), P, 15, None, A.bitwise_and)
-        ts(fc(0), I(18), -4.0, None, A.add)
-        ts(fc(1), I(19), -4.0, None, A.add)
-        copy(fc(4), I(21))
         ts(fc(5), I(21), -1.0, 1.0, A.mult, A.add)
-        ts(fc(6), I(21), float(ZC), None, A.mult)
-        ts(fc(7), I(21), -float(ZC), float(ZC), A.mult, A.add)
-        copy(fc(8), I(20))
+        copy(V("fc", 8, 10), V("ci", 20, 22))
+        ts(fc(1), I(19), -4.0, None, A.add)
+        copy(fc(0), I(18))
         ts(fc(3), I(18), fc(1), None, A.add)
-        ts(V("nl"), V("ci", 0, 16), fc(8), None, A.add)
-        holes("dn", V("nl"))
         copy(V("cu"), V("cfi"))
+
+    def lists():
+        act(fc(7), fc(5), float(ZC))
+        act(fc(6), fc(9), float(ZC))
+        act(V("nl"), V("nf"), func=AF.Identity, bias=fc(8))
+        holes("dn", V("nl"))
         holes("cd", V("cfi"))
 
     for t in range(ROUNDS):
@@ -226,9 +230,14 @@ def rank_program(g, core, T, topo):
         mm("p7", 128, ("x", 0), ("u", 0))
         mm("p6", 128, ("x", 128), ("u", 0))
         mm("p2", 256, ("us", 256), ("x", 0))
-        if t:
-            turn(V("tc"), V("vc"))
-            add_halves(V("cl"), "tc")
+        if t == 0:
+            ts(I(18), I(16), 7, None, A.bitwise_and)
+            ts(I(19), I(17), 4, None, A.arith_shift_right)
+            ts(I(20), I(16), 15, None, A.bitwise_and)
+            ts(I(21), I(16), 4, 1, A.arith_shift_right, A.bitwise_and)
+        else:
+            copy(V("cd"), V("tc", 0, 512, 16))
+            ts(V("cu"), V("cl"), -float(ZC), None, A.add)
         turn(V("owna"), V("p0", 0, 256))
         turn(V("ownb"), V("p1", 0, 256))
         tt(V("eqt", 0, 1024, 4), V("p0", 0, 256), V("owna"), A.is_equal)
@@ -243,9 +252,6 @@ def rank_program(g, core, T, topo):
         mm("p2", 256, ("hs", 0), ("h", 0))
         if t == 0:
             constants()
-        else:
-            copy(V("cu"), V("cl"))
-            holes("cd", V("cl"))
         for b in (0, 1):
             mm(("p5", "p6")[b], 256, ("eb", 128 * b), ("x", 0))
 
@@ -297,6 +303,10 @@ def rank_program(g, core, T, topo):
                     quant("w%d" % i, V(tile))
                     mm("p7", 256, ("sa", 0), ("w%d" % i, 0), i == 0, False)
         rest(ahead)
+        if t == 0:
+            lists()
+        for b, bank in enumerate(("p5", "p6")):
+            act(quarter("f", b), V(bank, 0, 256))
         for b in range(SPLIT // 2, 4):
             quant("w%d" % b, V("w%dt" % b))
             mm("p7", 256, ("sa", 0), ("w%d" % b, 0), False, False)
@@ -304,10 +314,11 @@ def rank_program(g, core, T, topo):
         mm("p7", 256, ("sa", 0), ("eq", 0), False, True)
         act(V("rk", 0, 256), V("p7", 0, 256), 2.0)
         act(V("vr"), V("rk"), lst=V("dn"))
-        for b in (2, 3):
-            mm(("p3", "p4")[b - 2], 256, ("eb", 128 * b), ("x", 0))
-        for b, bank in enumerate(("p5", "p6", "p3", "p4")):
+        for b, bank in ((2, "p3"), (3, "p4")):
+            mm(bank, 256, ("eb", 128 * b), ("x", 0))
             act(quarter("f", b), V(bank, 0, 256))
+        for b in range(4):
+            act(quarter("fh", b), quarter("f", b), lst=V("cu"))
         rest(levels(L1, L2))
         more = levels(L2, 7)
         next(more)
@@ -319,18 +330,15 @@ def rank_program(g, core, T, topo):
         rest(more)
         run("v", lambda: g.vector.tensor_copy(T["orow"][:, 0:256].indirect(T["rku"][:, :]), T["irow"][:, :]), [V("irow"), V("rku")], [V("orow", 0, 256)])
         act(V("vo"), V("orow"), lst=V("dn"))
-        for b in range(4):
-            act(quarter("fh", b), quarter("f", b), lst=V("cu"))
         act(V("orow", 256, 384), V("orow", 0, 128))
         act(V("sg", 0, 256), V("orow", 128, 384), lst=V("rku"))
         k = V("p0", 0, 256)
-        ts(V("nn"), k, V("fc", 0, 1), None, A.is_gt)
-        ts(V("mm"), k, V("fc", 1, 2), V("fc", 3, 4), A.max, A.is_equal)
+        ts(V("nn"), k, 4.0, fc(0), A.add, A.is_gt)
+        ts(V("mm"), k, fc(1), fc(3), A.max, A.is_equal)
         scan(V("cc"), V("nn"), V("nn"), A.mult, A.add)
         turn(V("to"), V("vo"))
         tt(V("cw", 0, 256), V("cc"), V("mm"), A.mult)
-        add_halves(V("ol"), "to")
-        holes("od", V("ol"))
+        copy(V("od"), V("to", 0, 512, 16))
         for half in (0, 1):
             act(V("vf", 256 * half, 256 * half + 256), V("cw"), lst=V("od", 16 * half, 16 * half + 16))
         if last:
@@ -338,9 +346,8 @@ def rank_program(g, core, T, topo):
             dma("y", T.op[:, :], T["crow"][0:128:16, :], [V("crow")], [])
         else:
             act(V("vc"), V("sg"), lst=V("cd"))
-        for b in range(4):
-            ts(V("xo", 16 * b, 16 * b + 16), V("rl"), 4.0, float(b), A.mult, A.add)
-        for half, tile in ((0, "et"), (1, "lt")):
+        add_halves(V("ol"), "to")
+        for half in (0, 1):
             a, z = 256 * half, 256 * half + 256
             if half == 0:
                 turn(V("tf", a, z), V("vf", a, z))
@@ -353,13 +360,13 @@ def rank_program(g, core, T, topo):
             for s in (0, 16):
                 tt(V("db", s + p, s + p + 8), V("ol", p, p + 8), V("da", s + p, s + p + 8), A.subtract)
             for s in (0, 16):
-                copy(V("lab", s + p, s + p + 8), V("db", s + p, s + p + 8))
+                ts(V("lab", s + p, s + p + 8), V("db", s + p, s + p + 8), -float(ZC), None, A.add)
             if half == 0:
                 turn(V("tf", 256, 512), V("vf", 256, 512))
             for b in range(4):
                 tmp = V("ta", 512 * half + 128 * b, 512 * half + 128 * b + 128)
                 act(tmp, quarter("fh", b), lst=V("lab", p, p + 8))
-                tt(V(tile, b, 512, 4), quarter("fh", b), tmp, A.add, lst=V("lab", 16 + p, 24 + p))
+                tt(V("et", b, 512, 4) if half == 0 else V("lt", 128 * b, 128 * b + 128), quarter("fh", b), tmp, A.add, lst=V("lab", 16 + p, 24 + p))
             if half == 0:
                 e = "e%d" % t
                 quant(e, V("et"))
@@ -369,20 +376,24 @@ def rank_program(g, core, T, topo):
                 g.remote_dma(T["ql%d" % t][:, 0:128].bitcast(dt.uint8), T["q" + e][:, 0:128].bitcast(dt.uint8), T.sem["ar%d" % t], T.sem["left"], pid, rid, m)
                 g.remote_dma(T["zl%d" % t][:, 0:128], T["z" + e][:, 0:128], T.sem["ar%d" % t], T.sem["left"], pid, rid, m)
                 total["left"] = total.get("left", 0) + 2 * len(topo.engines(core, nxt))
-                act(V("v32", 0, 512), V("et"), 32.0)
         ts(V("l32"), V("lt"), 32.0, None, A.mult)
+        for b in range(4):
+            act(V("v32", 256 * b, 256 * b + 128), V("et", b, 512, 4), 32.0)
         if last:
             quant("v", V("vt"))
+        else:
+            turn(V("tc"), V("vc"))
+            add_halves(V("cl"), "tc")
         n = 2 * len(topo.engines(prv, core))
         total["ar%d" % t] = n
         for z in ("ql%d" % t, "zl%d" % t):
             acc.setdefault(z, []).append((V(z), True, "r", "ar%d" % t, n, {}))
         for b, bank in enumerate(("p0", "p1", "p7", "p3")):
             mm(bank, 128, ("w", 128 * b), ("l%d" % t, 0))
-            tt(V("v32", 512 + b, 1024, 4), V(bank, 0, 128), V("l32", b, 512, 4), A.add)
+            tt(V("v32", 256 * b + 128, 256 * b + 256), V(bank, 0, 128), V("l32", 128 * b, 128 * b + 128), A.add)
         for b in range(4):
-            out, win, lst = V("xn", b, 1024, 4), V("v32"), V("xo", 16 * b, 16 * b + 16)
-            if b % 2 == 0:
+            out, win, lst = V("xn", b, 1024, 4), quarter("v32", b), V("rku")
+            if b in XS:
                 act(out, win, scale=0.03125, lst=lst)
             else:
                 ts(out, win, 0.03125, None, A.mult, lst=lst)

from concourse.mybir import dt, AluOpType as A, ActivationFunctionType as AF

ROUNDS = 3
ZC = 384
WIN = 400
XS = (0, 1)
SPLIT, L1, L2 = 4, 3, 5

SCRATCH = {}
PSUM = ["p%d" % i for i in range(8)]
for _n in PSUM:
    SCRATCH[_n] = ("psum", [128, 512], "float32")
for _n, _c in [("u", 128), ("v", 128), ("w", 512), ("us", 384), ("x", 256), ("eb", 512), ("sa", 128), ("k", 128), ("hs", 128), ("h", 256),
               ("w0", 256), ("w1", 256), ("w2", 256), ("w3", 256), ("eq", 256), ("kt1", 256), ("kt2", 256),
               ("e0", 128), ("e1", 128), ("e2", 128), ("l0", 128), ("l1", 128), ("l2", 128)]:
    SCRATCH["q" + _n] = ("sbuf", [128, _c], "float8_e4m3fn_x4")
    SCRATCH["z" + _n] = ("sbuf", [128, _c], "uint8")
for _d, _l in [("bfloat16", [("ut", 512), ("vt", 512), ("xt", 1024), ("xn", 1024), ("ebt", 528), ("half", 528), ("sat", 512), ("kt", 512), ("hst", 512),
                             ("ht", 1024), ("eqt", 1024), ("w0t", 1024), ("w1t", 1024), ("w2t", 1024), ("w3t", 1024), ("kt1t", 1024), ("kt2t", 1024),
                             ("rho", 256), ("st0", 256), ("st1", 256), ("f", 1024), ("fh", 1024), ("rk", WIN), ("orow", WIN), ("cw", WIN), ("sg", WIN),
                             ("vr", 512), ("vo", 512), ("vf", 512), ("vc", 512), ("tr", 512), ("to", 512), ("tf", 512), ("tc", 512),
                             ("r1", 256), ("r2", 128), ("r3", 64), ("nn", 256), ("mm", 256), ("cc", 256), ("irow", 256),
                             ("ta", 1024), ("et", 512), ("lt", 512), ("l32", 512), ("v32", 1024)]),
               ("float32", [("owna", 256), ("ownb", 256), ("crow", 256), ("ys", 256), ("fc", 16), ("nl", 16), ("nf", 16),
                            ("rl", 16), ("ol", 16), ("cl", 16), ("da", 32), ("db", 32)]),
               ("int32", [("ci", 32), ("cfi", 16), ("uli", 24)]),
               ("uint16", [("ul", 24), ("dn", 32), ("od", 32), ("cd", 32), ("cu", 16), ("rku", 16), ("lab", 32)])]:
    for _n, _c in _l:
        SCRATCH[_n] = ("sbuf", [128, _c], _d)

SEMAPHORES = ["cv", "cs", "ct", "cg", "left"] + ["ar%d" % t for t in range(ROUNDS)] + ["d%d" % i for i in range(20)]


def rank_program(g, core, T, topo):
    rank = T.rank_of(core)
    if rank is None:
        return
    nxt = T.cores[(rank + 1) % len(T.cores)]
    prv = T.cores[(rank - 1) % len(T.cores)]
    Q = {"v": g.vector, "s": g.scalar, "t": g.tensor, "g": g, "y": g.sync}
    SEM = {"v": "cv", "s": "cs", "t": "ct", "g": "cg"}
    total = {}
    know = {q: {} for q in Q}
    acc = {}
    dmas = [0]

    def V(name, lo=0, hi=None, st=1, p0=0, p1=128):
        return (name, lo, SCRATCH[name][1][1] if hi is None else hi, st, p0, p1)

    def ap(v):
        name, lo, hi, st, p0, p1 = v
        c = slice(lo, hi) if st == 1 else slice(lo, hi, st)
        return T[name][:, c] if (p0, p1) == (0, 128) else T[name][p0:p1, c]

    def meet(a, b):
        if a[4] >= b[5] or b[4] >= a[5] or a[1] >= b[2] or b[1] >= a[2]:
            return False
        return not (a[3] == b[3] and (a[1] - b[1]) % a[3])

    def learn(k, more):
        for s, n in more.items():
            if k.get(s, 0) < n:
                k[s] = n

    def order(q, reads, writes):
        for v, w in [(r, False) for r in reads] + [(r, True) for r in writes]:
            for (o, ow, oq, sem, n, kn) in acc.get(v[0], []):
                if v[0] in PSUM:
                    if not (w or ow or oq != q):
                        continue
                elif not (w or ow) or not meet(v, o):
                    continue
                if know[q].get(sem, 0) < n:
                    Q[q].wait_ge(T.sem[sem], n)
                    learn(know[q], {sem: n})
                    learn(know[q], kn)

    def note(q, reads, writes, sem, n):
        kn = dict(know[q])
        for v, w in [(r, False) for r in reads] + [(r, True) for r in writes]:
            L = acc.setdefault(v[0], [])
            if w:
                L[:] = [e for e in L if not (e[0][1] >= v[1] and e[0][2] <= v[2] and e[0][4] >= v[4] and e[0][5] <= v[5]
                                             and (v[3] == 1 or (v[3] == e[0][3] and (v[1] - e[0][1]) % v[3] == 0)))]
            L.append((v, w, q, sem, n, kn))

    def run(q, call, reads, writes, first=True):
        order(q, reads, writes if first else [])
        sem = SEM[q]
        if q == "g" and know[q].get(sem, 0) < total.get(sem, 0):
            g.wait_ge(T.sem[sem], total[sem])
            know[q][sem] = total[sem]
        call().then_inc(T.sem[sem], 1)
        total[sem] = total.get(sem, 0) + 1
        note(q, reads, writes, sem, total[sem])

    def dma(q, out, in_, reads, writes):
        order(q, reads, writes)
        sem = "d%d" % dmas[0]
        dmas[0] += 1
        Q[q].dma_start(out, in_).then_inc(T.sem[sem], 16)
        total[sem] = 16
        note(q, reads, writes, sem, 16)

    def ind(v, lst):
        return ap(v) if lst is None else ap(v).indirect(ap(lst))

    def some(*v):
        return [x for x in v if isinstance(x, tuple)]

    def col(s):
        return ap(s) if isinstance(s, tuple) else s

    def fill(v, c):
        run("v", lambda: g.vector.memset(ap(v), c), [], [v])

    def ts(out, in0, s1, s2, op0, op1=None, lst=None):
        a = [ap(out), ind(in0, lst), col(s1), col(s2), op0] + ([] if op1 is None else [op1])
        run("v", lambda: g.vector.tensor_scalar(*a), some(in0, s1, s2, lst), [out])

    def tt(out, in0, in1, op, lst=None):
        run("v", lambda: g.vector.tensor_tensor(ap(out), ind(in0, lst), ap(in1), op), some(in0, in1, lst), [out])

    def scan(out, d0, d1, op0, op1):
        run("v", lambda: g.vector.tensor_tensor_scan(ap(out), ap(d0), ap(d1), 0.0, op0, op1), [d0, d1], [out])

    def copy(out, in_):
        run("v", lambda: g.vector.tensor_copy(ap(out), ap(in_)), [in_], [out])

    def act(out, in_, scale=1.0, lst=None, func=AF.Copy, bias=None):
        k = {} if scale == 1.0 else {"scale": scale}
        if bias is not None:
            k["bias"] = ap(bias)
        run("s", lambda: g.scalar.activation(ap(out), ind(in_, lst), func, **k), some(in_, lst, bias), [out])

    def turn(out, in_):
        run("v", lambda: g.vector.transpose(ap(out), ap(in_)), [in_], [out])

    def quant(n, tile, lo=0, hi=None):
        c, z = V("q" + n, lo, hi), V("z" + n, lo, hi)
        run("v", lambda: g.vector.quantize_mx(ap(c), ap(z), ap(tile)), [tile], [c, z])

    def mm(bank, cols, L, R, start=True, stop=True):
        lc, lz = V("q" + L[0], L[1], L[1] + 128), V("z" + L[0], L[1], L[1] + 128)
        rc, rz = V("q" + R[0], R[1], R[1] + cols), V("z" + R[0], R[1], R[1] + cols)
        out = V(bank, 0, cols)
        run("t", lambda: g.tensor.matmul_mx(ap(out), ap(lc), ap(lz), ap(rc), ap(rz), start, stop), [lc, lz, rc, rz], [out], start)

    def add_halves(out, turned):
        tt(out, V(turned, 0, 512, 32), V(turned, 16, 512, 32), A.add)

    def holes(out, lst):
        ts(V(out, 0, 32, 2), lst, V("fc", 5, 6), V("fc", 6, 7), A.mult, A.add)
        ts(V(out, 1, 32, 2), lst, V("fc", 9, 10), V("fc", 7, 8), A.mult, A.add)

    def quarter(n, b):
        return V(n, 256 * b, 256 * b + 256)

    def I(i):
        return V("ci", i, i + 1)

    def fc(i):
        return V("fc", i, i + 1)

    dma("y", T["ut"][:, :], T.u[:, :], [], [V("ut")])
    dma("s", T["xt"][:, 0:512], T.x[:, 0:512], [], [V("xt", 0, 512)])
    dma("y", T["xt"][:, 512:1024], T.x[:, 512:1024], [], [V("xt", 512, 1024)])
    dma("y", T["cfi"][:, :], T.cf[:, :], [], [V("cfi")])
    dma("y", T["qw"][:, :].bitcast(dt.uint8), T.wc[:, :], [V("ut"), V("xt")], [V("qw")])
    dma("y", T["zw"][:, :], T.ws[:, :], [], [V("zw")])
    dma("y", T["vt"][:, :], T.v[:, :], [], [V("vt")])

    def iota(out, pattern, base, cm):
        run("g", lambda: g.iota(ap(out), pattern, base, cm), [], [out])

    iota(V("uli", 0, 8), [[32, 4], [0, 2]], 0, 0)
    iota(V("uli", 8, 16), [[32, 4], [0, 2]], 16, 0)
    iota(V("uli", 16, 24), [[0, 8]], 1, 0)
    iota(I(16), [[0, 1]], 0, 1)
    iota(I(17), [[0, 1]], 8, 1)
    run("g", lambda: g.iota(T["nf"][:, :], [[16, 16]], 0, 0, allow_small_or_imprecise_dtypes=True), [], [V("nf")])
    fill(V("half"), 0.5)
    fill(V("sat"), 0.0)
    run("g", lambda: g.affine_select(T["ebt"][:, :], T["half"][:, :], [[1, 528]], A.is_equal, 0.0, -4, -4), [V("half")], [V("ebt")])
    for a in range(4):
        for h in (0, 1):
            c = 128 * a + 64 * h
            o, i = V("sat", c, c + 64, 1, 32 * a, 32 * a + 32), V("half", c, c + 64, 1, 32 * a, 32 * a + 32)
            run("g", lambda: g.affine_select(ap(o), ap(i), [[0, 16], [1, 2], [0, 2]], A.is_equal, 0.0, -h, 0), [i], [o])
    run("g", lambda: g.iota(T["irow"][:, :], [[1, 256]], 0, 0, allow_small_or_imprecise_dtypes=True), [], [V("irow")])
    fill(V("hst"), 1.0 / 256)
    for b in (0, 1):
        act(V("kt", b, 512, 2), V("hst", b, 512, 2), (-2.0, 2.0)[b])
    fill(V("ht", 2, 1024, 4), 0.0)
    fill(V("ht", 3, 1024, 4), 0.0)
    fill(V("eqt", 1, 1024, 2), 0.0)
    copy(V("ul"), V("uli"))
    quant("hs", V("hst"))
    for n, c in (("rk", 0.0), ("orow", float(ZC)), ("cw", 0.0), ("sg", float(ZC))):
        fill(V(n, 256, WIN), c)
    fill(V("kt2t", 3, 1024, 4), 0.0)
    quant("u", V("ut"))
    run("v", lambda: g.vector.tensor_copy(T["qus"][:, 0:384].bitcast(dt.uint32), T["qu"][:, 0:128].bitcast(dt.uint32).indirect(T["ul"][:, 0:24])), [V("qu"), V("ul")], [V("qus")])
    run("s", lambda: g.scalar.activation(T["zus"][:, 0:384], T["zu"][:, 0:128].indirect(T["ul"][:, 0:24]), AF.Copy), [V("zu"), V("ul")], [V("zus")])

    def constants():
        quant("sa", V("sat"))
        quant("k", V("kt"))
        for b in range(4):
            quant("eb", V("ebt", 4 - b, 516 - b), 128 * b, 128 * b + 128)
        ts(fc(5), I(21), -1.0, 1.0, A.mult, A.add)
        copy(V("fc", 8, 10), V("ci", 20, 22))
        ts(fc(1), I(19), -4.0, None, A.add)
        copy(fc(0), I(18))
        ts(fc(3), I(18), fc(1), None, A.add)
        copy(V("cu"), V("cfi"))

    def lists():
        act(fc(7), fc(5), float(ZC))
        act(fc(6), fc(9), float(ZC))
        act(V("nl"), V("nf"), func=AF.Identity, bias=fc(8))
        holes("dn", V("nl"))
        holes("cd", V("cfi"))

    for t in range(ROUNDS):
        last = t == ROUNDS - 1
        quant("x", V("xt") if t == 0 else V("xn"))
        for bank, c in (("p0", 0), ("p1", 128), ("p3", 0), ("p4", 128)):
            mm(bank, 256, ("us", c), ("x", 0))
        mm("p7", 128, ("x", 0), ("u", 0))
        mm("p6", 128, ("x", 128), ("u", 0))
        mm("p2", 256, ("us", 256), ("x", 0))
        if t == 0:
            ts(I(18), I(16), 7, None, A.bitwise_and)
            ts(I(19), I(17), 4, None, A.arith_shift_right)
            ts(I(20), I(16), 15, None, A.bitwise_and)
            ts(I(21), I(16), 4, 1, A.arith_shift_right, A.bitwise_and)
        else:
            copy(V("cd"), V("tc", 0, 512, 16))
            ts(V("cu"), V("cl"), -float(ZC), None, A.add)
        turn(V("owna"), V("p0", 0, 256))
        turn(V("ownb"), V("p1", 0, 256))
        tt(V("eqt", 0, 1024, 4), V("p0", 0, 256), V("owna"), A.is_equal)
        tt(V("eqt", 2, 1024, 4), V("p1", 0, 256), V("ownb"), A.is_equal)
        for b in range(2):
            for a in range(4):
                v = V("eqt", 2 * b, 1024, 4, 32 * a, 32 * a + 32)
                run("g", lambda: g.affine_select(ap(v), ap(v), [[0, 8], [1, 32]], A.is_gt, 0.0, 0, -1), [v], [v])
        ts(V("ht", 0, 1024, 4), V("p2", 0, 256), V("p7", 1, 2), None, A.is_gt)
        ts(V("ht", 1, 1024, 4), V("p2", 0, 256), V("p6", 1, 2), None, A.is_gt)
        quant("h", V("ht"))
        mm("p2", 256, ("hs", 0), ("h", 0))
        if t == 0:
            constants()
        for b in (0, 1):
            mm(("p5", "p6")[b], 256, ("eb", 128 * b), ("x", 0))

        def level(m):
            S, flags = V("st%d" % (m % 2)), V("kt%dt" % (1 + m // 4), m % 4, 1024, 4)
            if m == 0:
                scan(S, V("rho"), V("rho"), A.max, A.max)
            else:
                ops = (A.max, A.min) if m % 2 else (A.min, A.max)
                scan(S, V("kt%dt" % (1 + (m - 1) // 4), (m - 1) % 4, 1024, 4), V("rho"), ops[0], ops[1])
            yield
            tt(flags, V("p2", 0, 256), S, A.not_equal if m % 2 else A.is_equal)
            yield
            if m in (3, 6):
                n = "kt%d" % (1 + m // 4)
                quant(n, V(n + "t"))
                mm("p0", 256, ("k", 0), (n, 0), m == 3, m == 6)

        def levels(a, z):
            for m in range(a, z):
                for _ in level(m):
                    yield

        def rest(it):
            for _ in it:
                pass
        ahead = levels(0, L1)
        for b in list(range(SPLIT, 8)) + list(range(SPLIT)):
            i = b // 2
            tile = "w%dt" % i
            for h in (0, 1):
                own, e, c = V(("owna", "ownb")[h], 32 * b, 32 * b + 1), 32 * b + 32, b % 2 + 2 * h
                left = V(tile, c, 4 * e, 4)
                if b < SPLIT:
                    ts(left, V(("p0", "p1")[h], 0, e), own, None, A.is_lt)
                else:
                    act(left, V(("p3", "p4")[h], 0, e), -1.0, None, AF.Relu, own)
                if b < 7:
                    ts(V(tile, 4 * e + c, 1024, 4), V(("p0", "p1")[h], e, 256), own, None, A.is_le)
                if b < SPLIT:
                    next(ahead, None)
            if b % 2:
                if b == SPLIT + 1:
                    act(V("rho"), V("p2", 0, 256))
                if b >= SPLIT:
                    w = V(tile, 0, 4 * e)
                    act(w, w, func=AF.Sign)
                else:
                    quant("w%d" % i, V(tile))
                    mm("p7", 256, ("sa", 0), ("w%d" % i, 0), i == 0, False)
        rest(ahead)
        if t == 0:
            lists()
        for b, bank in enumerate(("p5", "p6")):
            act(quarter("f", b), V(bank, 0, 256))
        for b in range(SPLIT // 2, 4):
            quant("w%d" % b, V("w%dt" % b))
            mm("p7", 256, ("sa", 0), ("w%d" % b, 0), False, False)
        quant("eq", V("eqt"))
        mm("p7", 256, ("sa", 0), ("eq", 0), False, True)
        act(V("rk", 0, 256), V("p7", 0, 256), 2.0)
        act(V("vr"), V("rk"), lst=V("dn"))
        for b, bank in ((2, "p3"), (3, "p4")):
            mm(bank, 256, ("eb", 128 * b), ("x", 0))
            act(quarter("f", b), V(bank, 0, 256))
        for b in range(4):
            act(quarter("fh", b), quarter("f", b), lst=V("cu"))
        rest(levels(L1, L2))
        more = levels(L2, 7)
        next(more)
        turn(V("tr"), V("vr"))
        next(more)
        add_halves(V("rl"), "tr")
        next(more)
        copy(V("rku"), V("rl"))
        rest(more)
        run("v", lambda: g.vector.tensor_copy(T["orow"][:, 0:256].indirect(T["rku"][:, :]), T["irow"][:, :]), [V("irow"), V("rku")], [V("orow", 0, 256)])
        act(V("vo"), V("orow"), lst=V("dn"))
        act(V("orow", 256, 384), V("orow", 0, 128))
        act(V("sg", 0, 256), V("orow", 128, 384), lst=V("rku"))
        k = V("p0", 0, 256)
        ts(V("nn"), k, 4.0, fc(0), A.add, A.is_gt)
        ts(V("mm"), k, fc(1), fc(3), A.max, A.is_equal)
        scan(V("cc"), V("nn"), V("nn"), A.mult, A.add)
        turn(V("to"), V("vo"))
        tt(V("cw", 0, 256), V("cc"), V("mm"), A.mult)
        copy(V("od"), V("to", 0, 512, 16))
        for half in (0, 1):
            act(V("vf", 256 * half, 256 * half + 256), V("cw"), lst=V("od", 16 * half, 16 * half + 16))
        if last:
            act(V("crow"), V("sg", 0, 256), lst=V("cu"))
            dma("y", T.op[:, :], T["crow"][0:128:16, :], [V("crow")], [])
        else:
            act(V("vc"), V("sg"), lst=V("cd"))
        add_halves(V("ol"), "to")
        for half in (0, 1):
            a, z = 256 * half, 256 * half + 256
            if half == 0:
                turn(V("tf", a, z), V("vf", a, z))
            for o, i in (("r1", "tf"), ("r2", "r1"), ("r3", "r2")):
                tt(V(o, a // 2, z // 2), V(i, a, z, 2), V(i, a + 1, z, 2), A.add)
                a, z = a // 2, z // 2
            p = 8 * half
            for s in (0, 1):
                tt(V("da", 16 * s + p, 16 * s + p + 8), V("r3", a + s, z, 4), V("r3", a + s + 2, z, 4), A.add)
            for s in (0, 16):
                tt(V("db", s + p, s + p + 8), V("ol", p, p + 8), V("da", s + p, s + p + 8), A.subtract)
            for s in (0, 16):
                ts(V("lab", s + p, s + p + 8), V("db", s + p, s + p + 8), -float(ZC), None, A.add)
            if half == 0:
                turn(V("tf", 256, 512), V("vf", 256, 512))
            for b in range(4):
                tmp = V("ta", 512 * half + 128 * b, 512 * half + 128 * b + 128)
                act(tmp, quarter("fh", b), lst=V("lab", p, p + 8))
                tt(V("et", b, 512, 4) if half == 0 else V("lt", 128 * b, 128 * b + 128), quarter("fh", b), tmp, A.add, lst=V("lab", 16 + p, 24 + p))
            if half == 0:
                e = "e%d" % t
                quant(e, V("et"))
                order("g", [V("q" + e), V("z" + e)], [])
                rid, pid = topo.addr(nxt)[:2]
                m = topo.mask(core, nxt)
                g.remote_dma(T["ql%d" % t][:, 0:128].bitcast(dt.uint8), T["q" + e][:, 0:128].bitcast(dt.uint8), T.sem["ar%d" % t], T.sem["left"], pid, rid, m)
                g.remote_dma(T["zl%d" % t][:, 0:128], T["z" + e][:, 0:128], T.sem["ar%d" % t], T.sem["left"], pid, rid, m)
                total["left"] = total.get("left", 0) + 2 * len(topo.engines(core, nxt))
        ts(V("l32"), V("lt"), 32.0, None, A.mult)
        for b in range(4):
            act(V("v32", 256 * b, 256 * b + 128), V("et", b, 512, 4), 32.0)
        if last:
            quant("v", V("vt"))
        else:
            turn(V("tc"), V("vc"))
            add_halves(V("cl"), "tc")
        n = 2 * len(topo.engines(prv, core))
        total["ar%d" % t] = n
        for z in ("ql%d" % t, "zl%d" % t):
            acc.setdefault(z, []).append((V(z), True, "r", "ar%d" % t, n, {}))
        for b, bank in enumerate(("p0", "p1", "p7", "p3")):
            mm(bank, 128, ("w", 128 * b), ("l%d" % t, 0))
            tt(V("v32", 256 * b + 128, 256 * b + 256), V(bank, 0, 128), V("l32", 128 * b, 128 * b + 128), A.add)
        for b in range(4):
            out, win, lst = V("xn", b, 1024, 4), quarter("v32", b), V("rku")
            if b in XS:
                act(out, win, scale=0.03125, lst=lst)
            else:
                ts(out, win, 0.03125, None, A.mult, lst=lst)

    quant("x", V("xn"))
    mm("p4", 256, ("v", 0), ("x", 0))
    copy(V("ys"), V("p4", 0, 256))
    dma("y", T.oc[:, :], T["qx"][:, :].bitcast(dt.uint8), [V("qx")], [])
    for i in range(4):
        dma("y" if i % 2 else "s", T.osc[4 * i:4 * i + 4, :], T["zx"][32 * i:32 * i + 4, :], [V("zx")], [])
    dma("y", T.y[:, :], T["ys"][:, :], [V("ys")], [])
    for sem, n in total.items():
        g.wait_ge(T.sem[sem], n)
